import numpy as np
import ml_dtypes


def mxq(x, axis, fmt="e4m3"):
    dtype, down = {"e4m3": (ml_dtypes.float8_e4m3fn, 7), "e5m2": (ml_dtypes.float8_e5m2, 14)}[fmt]
    v = np.moveaxis(np.asarray(x, np.float32).astype(ml_dtypes.bfloat16).astype(np.float64), axis, -1)
    blocks = v.reshape(v.shape[:-1] + (-1, 32))
    amax = np.abs(blocks).max(-1, keepdims=True)
    byte = np.maximum(np.where(amax > 0, np.frexp(amax)[1] - 1 + 127, 0) - down, 1)
    scale = np.exp2(byte - 127.0)
    codes = (blocks / scale).astype(np.float32).astype(dtype).astype(np.float64)
    return np.moveaxis((codes * scale).reshape(v.shape), -1, axis)


WIDE = False


def mx_kscale(k):
    if not WIDE:
        return np.ones(k)
    levels = np.array([10, -10, 5, -5, 0])
    if k % 512:
        return np.exp2(np.random.permutation(np.resize(levels, k // 32))).repeat(32)
    a = np.empty((k // 512, 16))
    for p in range(k // 512):
        a[p, :8] = np.random.permutation(np.resize(levels, 8))
        for g in range(8):
            far = levels[np.abs(levels - a[p, g]) >= 10]
            a[p, g + 8] = far[np.random.randint(len(far))]
    return np.exp2(a.ravel()).repeat(32)


def f64(x):
    return np.asarray(x).astype(np.float64)


def striped8(idx):
    return np.asarray(idx).reshape(8, -1, 16).transpose(0, 2, 1).reshape(128, -1).astype(np.uint16)


def unstriped8(offs):
    return offs.reshape(8, 16, -1).transpose(0, 2, 1).reshape(8, -1).astype(np.int64)


def pick8(x, idx, run):
    r = np.arange(len(x))
    return x[r[:, None], idx[r % (8 * run) // run]]


E2M1 = np.array([0.0, 0.5, 1.0, 1.5, 2.0, 3.0, 4.0, 6.0, -0.0, -0.5, -1.0, -1.5, -2.0, -3.0, -4.0, -6.0])


def pack_weight(w, fmt):
    k, n = w.shape
    w = f64(np.asarray(w, np.float32).astype(ml_dtypes.bfloat16)).reshape(k // 32, 32, n)
    amax = np.abs(w).max(1)
    if fmt == "e4m3":
        byte = np.frexp(amax)[1] - 1 + 127 - 7
    else:
        mant, ex = np.frexp(amax / 6.0)
        byte = np.where(mant > 0.5, ex, ex - 1) + 127
    byte = np.clip(np.where(amax > 0, byte, 1), 1, 254)
    scaled = (w * np.exp2(127.0 - byte)[:, None, :]).reshape(k, n).astype(np.float32)
    by_word = np.ascontiguousarray(scaled.reshape(k // 512, 128, 4, n).transpose(0, 1, 3, 2))
    if fmt == "e4m3":
        words = by_word.astype(ml_dtypes.float8_e4m3fn).view(np.uint8)
    else:
        c = by_word.astype(ml_dtypes.float4_e2m1fn).view(np.uint8) & 0xF
        words = (c[..., 0::2] | (c[..., 1::2] << 4)).reshape(k // 512, 128, 2 * n)
    return np.ascontiguousarray(words), np.ascontiguousarray(byte.astype(np.uint8).reshape(k // 512, 16, n))


def unpack_weight(words, scales, fmt):
    g, _, n = scales.shape
    words = np.ascontiguousarray(words).reshape(g, 128, n, -1)
    if fmt == "e4m3":
        vals = words.view(ml_dtypes.float8_e4m3fn).astype(np.float64)
    else:
        nib = np.empty((g, 128, n, 4), np.uint8)
        nib[..., 0::2] = words & 0xF
        nib[..., 1::2] = words >> 4
        vals = E2M1[nib]
    vals = vals * np.repeat(np.exp2(scales.astype(np.float64) - 127.0), 8, axis=1)[..., None]
    return vals.transpose(0, 1, 3, 2).reshape(g * 512, n)


def sigmoid(v):
    return 1.0 / (1.0 + np.exp(-v))


D, E, T, Q, I = 512, 512, 1024, 128, 512


def setup_inputs():
    n = np.random.standard_normal
    idx = np.stack([np.random.permutation(T)[:I] for _ in range(8)])
    fd = mx_kscale(D)
    fe = mx_kscale(E)
    keysp = pack_weight(n((D, T)) / fd[:, None], "e2m1")
    return {
        "query": (n((D, Q)) * 0.5 / np.sqrt(D) * fd[:, None]).astype(np.float32),
        "keys_words": keysp[0],
        "keys_scales": keysp[1],
        "gout": (n((E, Q)) * 1 / np.sqrt(E) * fe[:, None]).astype(np.float32),
        "vals": (n((E, T)) / fe[:, None]).astype(np.float32),
        "lse": (np.random.uniform(6.8, 7.2, (Q, 1))).astype(np.float32),
        "delta": (np.random.uniform(-0.3, 0.3, (Q, 1))).astype(np.float32),
        "steep": (np.random.uniform(2.0, 6.0, (Q, 1))).astype(np.float32),
        "old": (0.5 * n((Q, I))).astype(np.float32),
        "offs": striped8(idx),
    }


def reference(query, keys_words, keys_scales, gout, vals, lse, delta, steep, old, offs):
    idx = unstriped8(offs)
    keysu = unpack_weight(keys_words, keys_scales, "e2m1")
    queryq = mxq(f64(query), 0, "e4m3")
    a = queryq.T @ keysu
    goutq = mxq(f64(gout), 0, "e4m3")
    valsq = mxq(f64(vals), 0, "e4m3")
    dp = goutq.T @ valsq
    ds = np.exp(a - f64(lse)) * (dp - f64(delta)) * 1024.0
    y = pick8(ds, idx, 16) * sigmoid(pick8(a, idx, 16) * f64(steep)) + f64(old)
    return y

@@ -1,0 +1,144 @@
+import math
+from contextlib import ExitStack
+
+import concourse.mybir as mybir
+
+D, E, T, Q, I = 512, 512, 1024, 128, 512
+FLOPS = 2 * Q * T * (D + E)
+
+F32 = mybir.dt.float32
+BF16 = mybir.dt.bfloat16
+I32 = mybir.dt.int32
+U32 = mybir.dt.uint32
+U16 = mybir.dt.uint16
+U8 = mybir.dt.uint8
+FP8X4 = mybir.dt.float8_e4m3fn_x4
+FP4X4 = mybir.dt.float4_e2m1fn_x4
+ALU = mybir.AluOpType
+ACT = mybir.ActivationFunctionType
+
+P = 128
+PACK = 4
+BANK = 512
+CHUNKS = (256, 256, 256, 256)
+PIECES = (256, 256)
+
+
+def tile_attend_gboost_heads_kernel(tc, query, keys_words, keys_scales, gout, vals, lse, delta, steep, old, offs, out):
+    nc = tc.nc
+    with ExitStack() as ctx:
+        keep = ctx.enter_context(tc.tile_pool(name="keep", bufs=1))
+        psum = ctx.enter_context(tc.psum_pool(name="psum", bufs=1))
+
+        def load_rows(rows, name):
+            raw = keep.tile([P, PACK, rows.shape[1]], F32, name=name)
+            nc.sync.dma_start(out=raw[:], in_=rows.rearrange("(p j) w -> p j w", j=PACK))
+            return raw
+
+        def interleave(copy, raw, name):
+            grouped = keep.tile([P, raw.shape[2], PACK], BF16, name=name, align_bytes=64)
+            copy(
+                out=grouped[:].rearrange("p (c i) j -> p c j i", i=4),
+                in_=raw[:].rearrange("p j (c i) -> p c j i", i=4),
+            )
+            return grouped
+
+        def quantize(grouped, name):
+            width = grouped.shape[1]
+            codes = keep.tile([P, width], U32, name=name + "_codes", align_bytes=64)
+            scales = keep.tile([P, width], U8, name=name + "_scales", align_bytes=64)
+            nc.vector.quantize_mx(
+                out=codes[:].bitcast(FP8X4), scales=scales[:], in_=grouped[:].rearrange("p w j -> p (w j)")
+            )
+            return codes, scales
+
+        def load_column(column, name):
+            tile = keep.tile([P, 1], F32, name=name)
+            nc.sync.dma_start(out=tile[:], in_=column)
+            return tile
+
+        key_scales = keep.tile([P, T], U8, name="key_scales", align_bytes=64)
+        nc.vector.memset(key_scales[:].bitcast(I32), 0)
+
+        query_raw = load_rows(query, "query_raw")
+        for quadrant in range(4):
+            nc.scalar.dma_start(
+                out=key_scales[32 * quadrant : 32 * quadrant + 4, :].bitcast(I32),
+                in_=keys_scales[0, 4 * quadrant : 4 * quadrant + 4, :].bitcast(I32),
+            )
+        key_words = keep.tile([P, 2 * T], U8, name="key_words", align_bytes=64)
+        nc.sync.dma_start(out=key_words[:].bitcast(I32), in_=keys_words[0].bitcast(I32))
+        gout_raw = load_rows(gout, "gout_raw")
+        starts = [sum(CHUNKS[:c]) for c in range(len(CHUNKS))]
+        vals_raw = []
+        vals_raw.append(load_rows(vals[:, starts[0] : starts[0] + CHUNKS[0]], "vals_raw0"))
+        lse_sb = load_column(lse, "lse_sb")
+        vals_raw.append(load_rows(vals[:, starts[1] : starts[1] + CHUNKS[1]], "vals_raw1"))
+        delta_sb = load_column(delta, "delta_sb")
+        steep_sb = load_column(steep, "steep_sb")
+        offsets = keep.tile([P, I // 16], U16, name="offsets")
+        nc.sync.dma_start(offsets[:], offs)
+        for c in range(2, len(CHUNKS)):
+            vals_raw.append(load_rows(vals[:, starts[c] : starts[c] + CHUNKS[c]], "vals_raw%d" % c))
+        old_sb = keep.tile([P, I], F32, name="old_sb")
+        nc.sync.dma_start(out=old_sb[:], in_=old)
+
+        query_codes, query_scales = quantize(interleave(nc.vector.tensor_copy, query_raw, "query_bf"), "query")
+        gout_codes, gout_scales = quantize(interleave(nc.scalar.copy, gout_raw, "gout_bf"), "gout")
+
+        exp_bias = keep.tile([P, 1], F32, name="exp_bias")
+        nc.vector.tensor_scalar(exp_bias[:], lse_sb[:], -1.0, math.log(1024.0), ALU.mult, ALU.add)
+
+        scores = keep.tile([P, T], F32, name="scores")
+        weights = keep.tile([P, T], F32, name="weights")
+        for half in range(T // BANK):
+            cols = slice(half * BANK, (half + 1) * BANK)
+            bank = psum.tile([P, BANK], F32, name="score_bank%d" % half)
+            nc.tensor.matmul_mx(
+                out=bank[:],
+                lhsT=query_codes[:].bitcast(FP8X4),
+                lhsT_scale=query_scales[:],
+                rhs=key_words[:, 2 * half * BANK : 2 * (half + 1) * BANK].bitcast(FP4X4),
+                rhs_scale=key_scales[:, cols],
+                start=True,
+                stop=True,
+            )
+            nc.scalar.activation(weights[:, cols], bank[:], ACT.Exp, bias=exp_bias[:])
+            nc.scalar.copy(scores[:, cols], bank[:])
+
+        steepened = keep.tile([P, I], F32, name="steepened")
+        nc.scalar.activation(steepened[:], scores[:].indirect(offsets[:]), ACT.Copy, scale=steep_sb[:])
+        half_tanh = keep.tile([P, I], F32, name="half_tanh")
+        nc.scalar.activation(half_tanh[:], steepened[:], ACT.Tanh, scale=0.5)
+        gate = keep.tile([P, I], F32, name="gate")
+        nc.scalar.activation(gate[:], half_tanh[:], ACT.Copy, scale=0.5, bias=0.5)
+
+        grads = keep.tile([P, T], F32, name="grads")
+        for c, width in enumerate(CHUNKS):
+            cols = slice(starts[c], starts[c] + width)
+            codes, scales = quantize(interleave(nc.vector.tensor_copy, vals_raw[c], "vals_bf%d" % c), "vals%d" % c)
+            bank = psum.tile([P, width], F32, name="grad_bank%d" % c)
+            nc.tensor.matmul_mx(
+                out=bank[:],
+                lhsT=gout_codes[:].bitcast(FP8X4),
+                lhsT_scale=gout_scales[:],
+                rhs=codes[:].bitcast(FP8X4),
+                rhs_scale=scales[:],
+                start=True,
+                stop=True,
+            )
+            nc.vector.scalar_tensor_tensor(
+                grads[:, cols], bank[:], delta_sb[:], weights[:, cols], ALU.subtract, ALU.mult
+            )
+
+        first = 0
+        for n, width in enumerate(PIECES):
+            slots = slice(first, first + width)
+            gated = keep.tile([P, width], F32, name="gated%d" % n)
+            nc.vector.tensor_tensor(
+                gated[:], grads[:].indirect(offsets[:, first // 16 : (first + width) // 16]), gate[:, slots], ALU.mult
+            )
+            total = keep.tile([P, width], F32, name="total%d" % n)
+            nc.vector.tensor_tensor(total[:], gated[:], old_sb[:, slots], ALU.add)
+            nc.sync.dma_start(out=out[:, slots], in_=total[:])
+            first = first + width

@@ -20,8 +20,8 @@ ACT = mybir.ActivationFunctionType
 P = 128
 PACK = 4
 BANK = 512
-CHUNKS = (256, 256, 256, 256)
-PIECES = (256, 256)
+CHUNKS = (128, 256, 256, 256, 128)
+HALF = I // 2
 
 
 def tile_attend_gboost_heads_kernel(tc, query, keys_words, keys_scales, gout, vals, lse, delta, steep, old, offs, out):
@@ -31,7 +31,7 @@ def tile_attend_gboost_heads_kernel(tc, query, keys_words, keys_scales, gout, va
         psum = ctx.enter_context(tc.psum_pool(name="psum", bufs=1))
 
         def load_rows(rows, name):
-            raw = keep.tile([P, PACK, rows.shape[1]], F32, name=name)
+            raw = keep.tile([P, PACK, rows.shape[1]], F32, name=name, tag=name)
             nc.sync.dma_start(out=raw[:], in_=rows.rearrange("(p j) w -> p j w", j=PACK))
             return raw
 
@@ -57,37 +57,43 @@ def tile_attend_gboost_heads_kernel(tc, query, keys_words, keys_scales, gout, va
             nc.sync.dma_start(out=tile[:], in_=column)
             return tile
 
-        key_scales = keep.tile([P, T], U8, name="key_scales", align_bytes=64)
-        nc.vector.memset(key_scales[:].bitcast(I32), 0)
+        key_scales = keep.tile([P, 4 * T], U8, name="key_scales", align_bytes=64)
+        nc.sync.dma_start(
+            out=key_scales[0:4, :].bitcast(I32).rearrange("r (q c) -> r q c", q=4),
+            in_=keys_scales[0].bitcast(I32).rearrange("(q r) c -> r q c", q=4),
+        )
+
+        starts = [sum(CHUNKS[:c]) for c in range(len(CHUNKS))]
+
+        def load_vals(c):
+            return load_rows(vals[:, starts[c] : starts[c] + CHUNKS[c]], "vals_raw%d" % c)
 
         query_raw = load_rows(query, "query_raw")
-        for quadrant in range(4):
-            nc.scalar.dma_start(
-                out=key_scales[32 * quadrant : 32 * quadrant + 4, :].bitcast(I32),
-                in_=keys_scales[0, 4 * quadrant : 4 * quadrant + 4, :].bitcast(I32),
-            )
         key_words = keep.tile([P, 2 * T], U8, name="key_words", align_bytes=64)
         nc.sync.dma_start(out=key_words[:].bitcast(I32), in_=keys_words[0].bitcast(I32))
-        gout_raw = load_rows(gout, "gout_raw")
-        starts = [sum(CHUNKS[:c]) for c in range(len(CHUNKS))]
-        vals_raw = []
-        vals_raw.append(load_rows(vals[:, starts[0] : starts[0] + CHUNKS[0]], "vals_raw0"))
         lse_sb = load_column(lse, "lse_sb")
-        vals_raw.append(load_rows(vals[:, starts[1] : starts[1] + CHUNKS[1]], "vals_raw1"))
+        gout_raw = load_rows(gout, "gout_raw")
+        vals_raw = [load_vals(0)]
         delta_sb = load_column(delta, "delta_sb")
+        vals_raw.append(load_vals(1))
         steep_sb = load_column(steep, "steep_sb")
         offsets = keep.tile([P, I // 16], U16, name="offsets")
         nc.sync.dma_start(offsets[:], offs)
-        for c in range(2, len(CHUNKS)):
-            vals_raw.append(load_rows(vals[:, starts[c] : starts[c] + CHUNKS[c]], "vals_raw%d" % c))
+        vals_raw.extend(load_vals(c) for c in range(2, len(CHUNKS)))
         old_sb = keep.tile([P, I], F32, name="old_sb")
         nc.sync.dma_start(out=old_sb[:], in_=old)
 
+        for quadrant in range(1, 4):
+            nc.vector.tensor_copy(
+                key_scales[32 * quadrant : 32 * quadrant + 4, 0:T].bitcast(I32),
+                key_scales[0:4, quadrant * T : (quadrant + 1) * T].bitcast(I32),
+            )
+
         query_codes, query_scales = quantize(interleave(nc.vector.tensor_copy, query_raw, "query_bf"), "query")
-        gout_codes, gout_scales = quantize(interleave(nc.scalar.copy, gout_raw, "gout_bf"), "gout")
+        gout_codes, gout_scales = quantize(interleave(nc.vector.tensor_copy, gout_raw, "gout_bf"), "gout")
 
         exp_bias = keep.tile([P, 1], F32, name="exp_bias")
-        nc.vector.tensor_scalar(exp_bias[:], lse_sb[:], -1.0, math.log(1024.0), ALU.mult, ALU.add)
+        nc.scalar.activation(exp_bias[:], lse_sb[:], ACT.Copy, scale=-1.0, bias=math.log(1024.0))
 
         scores = keep.tile([P, T], F32, name="scores")
         weights = keep.tile([P, T], F32, name="weights")
@@ -110,14 +116,22 @@ def tile_attend_gboost_heads_kernel(tc, query, keys_words, keys_scales, gout, va
         nc.scalar.activation(steepened[:], scores[:].indirect(offsets[:]), ACT.Copy, scale=steep_sb[:])
         half_tanh = keep.tile([P, I], F32, name="half_tanh")
         nc.scalar.activation(half_tanh[:], steepened[:], ACT.Tanh, scale=0.5)
-        gate = keep.tile([P, I], F32, name="gate")
-        nc.scalar.activation(gate[:], half_tanh[:], ACT.Copy, scale=0.5, bias=0.5)
+        gate = keep.tile([P, HALF], F32, name="gate")
+        nc.scalar.activation(gate[:], half_tanh[:, 0:HALF], ACT.Copy, scale=0.5, bias=0.5)
 
-        grads = keep.tile([P, T], F32, name="grads")
+        banks = []
+
+        def score_gradient(c):
+            cols = slice(starts[c], starts[c] + CHUNKS[c])
+            nc.vector.scalar_tensor_tensor(
+                grads[:, cols], banks[c][:], delta_sb[:], weights[:, cols], ALU.subtract, ALU.mult
+            )
+
         for c, width in enumerate(CHUNKS):
-            cols = slice(starts[c], starts[c] + width)
-            codes, scales = quantize(interleave(nc.vector.tensor_copy, vals_raw[c], "vals_bf%d" % c), "vals%d" % c)
+            grouped = interleave(nc.vector.tensor_copy, vals_raw[c], "vals_bf%d" % c)
+            codes, scales = quantize(grouped, "vals%d" % c)
             bank = psum.tile([P, width], F32, name="grad_bank%d" % c)
+            banks.append(bank)
             nc.tensor.matmul_mx(
                 out=bank[:],
                 lhsT=gout_codes[:].bitcast(FP8X4),
@@ -127,18 +141,22 @@ def tile_attend_gboost_heads_kernel(tc, query, keys_words, keys_scales, gout, va
                 start=True,
                 stop=True,
             )
-            nc.vector.scalar_tensor_tensor(
-                grads[:, cols], bank[:], delta_sb[:], weights[:, cols], ALU.subtract, ALU.mult
-            )
+        grads = keep.tile([P, T], F32, name="grads", tag="vals_raw3")
+        for c in range(len(CHUNKS)):
+            score_gradient(c)
 
-        first = 0
-        for n, width in enumerate(PIECES):
-            slots = slice(first, first + width)
-            gated = keep.tile([P, width], F32, name="gated%d" % n)
-            nc.vector.tensor_tensor(
-                gated[:], grads[:].indirect(offsets[:, first // 16 : (first + width) // 16]), gate[:, slots], ALU.mult
-            )
-            total = keep.tile([P, width], F32, name="total%d" % n)
-            nc.vector.tensor_tensor(total[:], gated[:], old_sb[:, slots], ALU.add)
-            nc.sync.dma_start(out=out[:, slots], in_=total[:])
-            first = first + width
+        gated = keep.tile([P, HALF], F32, name="gated")
+        for first in range(0, HALF, HALF // 2):
+            slots = slice(first, first + HALF // 2)
+            listed = grads[:].indirect(offsets[:, slots.start // 16 : slots.stop // 16])
+            nc.vector.tensor_tensor(gated[:, slots], listed, gate[:, slots], ALU.mult)
+        picked = keep.tile([P, HALF], F32, name="picked", tag="picked")
+        nc.scalar.activation(picked[:], grads[:].indirect(offsets[:, HALF // 16 : I // 16]), ACT.Copy)
+        doubled = keep.tile([P, HALF], F32, name="doubled")
+        nc.vector.scalar_tensor_tensor(doubled[:], half_tanh[:, HALF:I], 1.0, picked[:], ALU.add, ALU.mult)
+        low = keep.tile([P, HALF], F32, name="low", tag="low")
+        nc.vector.tensor_tensor(low[:], gated[:], old_sb[:, 0:HALF], ALU.add)
+        nc.sync.dma_start(out=out[:, 0:HALF], in_=low[:])
+        high = keep.tile([P, HALF], F32, name="high")
+        nc.vector.scalar_tensor_tensor(high[:], doubled[:], 0.5, old_sb[:, HALF:I], ALU.mult, ALU.add)
+        nc.scalar.dma_start(out=out[:, HALF:I], in_=high[:])

import math
from contextlib import ExitStack

import concourse.mybir as mybir

D, E, T, Q, I = 512, 512, 1024, 128, 512
FLOPS = 2 * Q * T * (D + E)

F32 = mybir.dt.float32
BF16 = mybir.dt.bfloat16
I32 = mybir.dt.int32
U32 = mybir.dt.uint32
U16 = mybir.dt.uint16
U8 = mybir.dt.uint8
FP8X4 = mybir.dt.float8_e4m3fn_x4
FP4X4 = mybir.dt.float4_e2m1fn_x4
ALU = mybir.AluOpType
ACT = mybir.ActivationFunctionType

P = 128
PACK = 4
BANK = 512
CHUNKS = (128, 256, 256, 256, 128)
HALF = I // 2


def tile_attend_gboost_heads_kernel(tc, query, keys_words, keys_scales, gout, vals, lse, delta, steep, old, offs, out):
    nc = tc.nc
    with ExitStack() as ctx:
        keep = ctx.enter_context(tc.tile_pool(name="keep", bufs=1))
        psum = ctx.enter_context(tc.psum_pool(name="psum", bufs=1))

        def load_rows(rows, name):
            raw = keep.tile([P, PACK, rows.shape[1]], F32, name=name, tag=name)
            nc.sync.dma_start(out=raw[:], in_=rows.rearrange("(p j) w -> p j w", j=PACK))
            return raw

        def interleave(copy, raw, name):
            grouped = keep.tile([P, raw.shape[2], PACK], BF16, name=name, align_bytes=64)
            copy(
                out=grouped[:].rearrange("p (c i) j -> p c j i", i=4),
                in_=raw[:].rearrange("p j (c i) -> p c j i", i=4),
            )
            return grouped

        def quantize(grouped, name):
            width = grouped.shape[1]
            codes = keep.tile([P, width], U32, name=name + "_codes", align_bytes=64)
            scales = keep.tile([P, width], U8, name=name + "_scales", align_bytes=64)
            nc.vector.quantize_mx(
                out=codes[:].bitcast(FP8X4), scales=scales[:], in_=grouped[:].rearrange("p w j -> p (w j)")
            )
            return codes, scales

        def load_column(column, name):
            tile = keep.tile([P, 1], F32, name=name)
            nc.sync.dma_start(out=tile[:], in_=column)
            return tile

        key_scales = keep.tile([P, 4 * T], U8, name="key_scales", align_bytes=64)
        nc.sync.dma_start(
            out=key_scales[0:4, :].bitcast(I32).rearrange("r (q c) -> r q c", q=4),
            in_=keys_scales[0].bitcast(I32).rearrange("(q r) c -> r q c", q=4),
        )

        starts = [sum(CHUNKS[:c]) for c in range(len(CHUNKS))]

        def load_vals(c):
            return load_rows(vals[:, starts[c] : starts[c] + CHUNKS[c]], "vals_raw%d" % c)

        query_raw = load_rows(query, "query_raw")
        key_words = keep.tile([P, 2 * T], U8, name="key_words", align_bytes=64)
        nc.sync.dma_start(out=key_words[:].bitcast(I32), in_=keys_words[0].bitcast(I32))
        lse_sb = load_column(lse, "lse_sb")
        gout_raw = load_rows(gout, "gout_raw")
        vals_raw = [load_vals(0)]
        delta_sb = load_column(delta, "delta_sb")
        vals_raw.append(load_vals(1))
        steep_sb = load_column(steep, "steep_sb")
        offsets = keep.tile([P, I // 16], U16, name="offsets")
        nc.sync.dma_start(offsets[:], offs)
        vals_raw.extend(load_vals(c) for c in range(2, len(CHUNKS)))
        old_sb = keep.tile([P, I], F32, name="old_sb")
        nc.sync.dma_start(out=old_sb[:], in_=old)

        for quadrant in range(1, 4):
            nc.vector.tensor_copy(
                key_scales[32 * quadrant : 32 * quadrant + 4, 0:T].bitcast(I32),
                key_scales[0:4, quadrant * T : (quadrant + 1) * T].bitcast(I32),
            )

        query_codes, query_scales = quantize(interleave(nc.vector.tensor_copy, query_raw, "query_bf"), "query")
        gout_codes, gout_scales = quantize(interleave(nc.vector.tensor_copy, gout_raw, "gout_bf"), "gout")

        exp_bias = keep.tile([P, 1], F32, name="exp_bias")
        nc.scalar.activation(exp_bias[:], lse_sb[:], ACT.Copy, scale=-1.0, bias=math.log(1024.0))

        scores = keep.tile([P, T], F32, name="scores")
        weights = keep.tile([P, T], F32, name="weights")
        for half in range(T // BANK):
            cols = slice(half * BANK, (half + 1) * BANK)
            bank = psum.tile([P, BANK], F32, name="score_bank%d" % half)
            nc.tensor.matmul_mx(
                out=bank[:],
                lhsT=query_codes[:].bitcast(FP8X4),
                lhsT_scale=query_scales[:],
                rhs=key_words[:, 2 * half * BANK : 2 * (half + 1) * BANK].bitcast(FP4X4),
                rhs_scale=key_scales[:, cols],
                start=True,
                stop=True,
            )
            nc.scalar.activation(weights[:, cols], bank[:], ACT.Exp, bias=exp_bias[:])
            nc.scalar.copy(scores[:, cols], bank[:])

        steepened = keep.tile([P, I], F32, name="steepened")
        nc.scalar.activation(steepened[:], scores[:].indirect(offsets[:]), ACT.Copy, scale=steep_sb[:])
        half_tanh = keep.tile([P, I], F32, name="half_tanh")
        nc.scalar.activation(half_tanh[:], steepened[:], ACT.Tanh, scale=0.5)
        gate = keep.tile([P, HALF], F32, name="gate")
        nc.scalar.activation(gate[:], half_tanh[:, 0:HALF], ACT.Copy, scale=0.5, bias=0.5)

        banks = []

        def score_gradient(c):
            cols = slice(starts[c], starts[c] + CHUNKS[c])
            nc.vector.scalar_tensor_tensor(
                grads[:, cols], banks[c][:], delta_sb[:], weights[:, cols], ALU.subtract, ALU.mult
            )

        for c, width in enumerate(CHUNKS):
            grouped = interleave(nc.vector.tensor_copy, vals_raw[c], "vals_bf%d" % c)
            codes, scales = quantize(grouped, "vals%d" % c)
            bank = psum.tile([P, width], F32, name="grad_bank%d" % c)
            banks.append(bank)
            nc.tensor.matmul_mx(
                out=bank[:],
                lhsT=gout_codes[:].bitcast(FP8X4),
                lhsT_scale=gout_scales[:],
                rhs=codes[:].bitcast(FP8X4),
                rhs_scale=scales[:],
                start=True,
                stop=True,
            )
        grads = keep.tile([P, T], F32, name="grads", tag="vals_raw3")
        for c in range(len(CHUNKS)):
            score_gradient(c)

        gated = keep.tile([P, HALF], F32, name="gated")
        for first in range(0, HALF, HALF // 2):
            slots = slice(first, first + HALF // 2)
            listed = grads[:].indirect(offsets[:, slots.start // 16 : slots.stop // 16])
            nc.vector.tensor_tensor(gated[:, slots], listed, gate[:, slots], ALU.mult)
        picked = keep.tile([P, HALF], F32, name="picked", tag="picked")
        nc.scalar.activation(picked[:], grads[:].indirect(offsets[:, HALF // 16 : I // 16]), ACT.Copy)
        doubled = keep.tile([P, HALF], F32, name="doubled")
        nc.vector.scalar_tensor_tensor(doubled[:], half_tanh[:, HALF:I], 1.0, picked[:], ALU.add, ALU.mult)
        low = keep.tile([P, HALF], F32, name="low", tag="low")
        nc.vector.tensor_tensor(low[:], gated[:], old_sb[:, 0:HALF], ALU.add)
        nc.sync.dma_start(out=out[:, 0:HALF], in_=low[:])
        high = keep.tile([P, HALF], F32, name="high")
        nc.vector.scalar_tensor_tensor(high[:], doubled[:], 0.5, old_sb[:, HALF:I], ALU.mult, ALU.add)
        nc.scalar.dma_start(out=out[:, HALF:I], in_=high[:])
